import numpy as np, ml_dtypes
CORES = [7,39,87,119,135,167,215,247,263,295,343,375,391,423,471,503]
N = 16
import mx_ref
NC = 128
BF = ml_dtypes.bfloat16
def setup_inputs(rng):
    def f(*shape):
        return mx_ref.flush((rng.standard_normal(shape, dtype=np.float32) * np.exp2(rng.integers(-2, 3, shape[:-1] + (1,)))).astype(BF))
    return {"c": f(N, 128, 512), "x": f(N, 128, 4 * NC)}
def setup_inputs_blocks(rng):
    d = setup_inputs(rng)
    for k in ("c", "x"): d[k] = mx_ref.spread(d[k], rng, 2)
    return d
def setup_inputs_wide(rng):
    d = setup_inputs(rng)
    for k in ("c", "x"): d[k] = mx_ref.flush((d[k].astype(np.float32) * np.exp2(rng.integers(-8, 9, (N, 1, 1))).astype(np.float32)).astype(BF))
    return d
def setup_inputs_zeros(rng):
    d = setup_inputs(rng); v = d["x"].reshape(N, 128, -1, 4).copy()
    v[np.broadcast_to((rng.random((N, 1, v.shape[2], 1)) < 0.33), v.shape)] = 0
    d["x"] = v.reshape(d["x"].shape)
    return d
def reference(c, x):
    QC = [mx_ref.quantize(c[k]) for k in range(N)]; QX = [mx_ref.quantize(x[j]) for j in range(N)]
    y = np.zeros((N, 128, NC), np.float32)
    for r in range(N):
        for j in range(N):
            p = mx_ref.matmul(QC[(r - j) % N], QX[j])
            y[r] = p if j == 0 else y[r] + p
    return {"y": y}

@@ -1,0 +1,168 @@
+from concourse.bass import DstId, RemoteDMATransfer
+from concourse.mybir import dt
+
+N = 16
+WORLD = 512
+HALF = 128
+SLOT = 2 * HALF
+DIRECT = 2
+FORWARD = 2
+
+SCRATCH = {
+    "cb": ("sbuf", [128, 4 * HALF], "bfloat16"),
+    "xb": ("sbuf", [128, 4 * HALF], "bfloat16"),
+    "q": ("sbuf", [128, N * SLOT], "float8_e4m3fn_x4"),
+    "s": ("sbuf", [128, N * SLOT], "uint8"),
+    "yb": ("sbuf", [128, HALF], "float32"),
+    "acc": ("psum", [128, 512], "float32"),
+}
+SEMAPHORES = ["ldc", "ldx", "qd", "sent", "mm", "cp", "st"] + ["a%d" % j for j in range(N)]
+
+ROW, HOP = 512, 60000
+
+_CACHE = {}
+
+
+def _bits(m):
+    return [i for i in range(16) if (m >> i) & 1]
+
+
+def _build(cores, topo):
+    n = len(cores)
+    rk = [topo.rack(topo.host(c)) for c in cores]
+    partner = {}
+    for r, c in enumerate(cores):
+        for r2, c2 in enumerate(cores):
+            if rk[r2] != rk[r] and topo.chip(c2) == topo.chip(c) and topo.may_write(c, c2):
+                partner[r] = r2
+    pos, at = {}, {}
+    for i, r in enumerate([r for r in range(n) if rk[r] == rk[0]]):
+        pos[r] = i
+        pos[partner[r]] = i
+    for r in range(n):
+        at[(rk[r], pos[r])] = r
+    per = n // 2
+    near, far = {}, {}
+    for r, c in enumerate(cores):
+        mates = [w for w in range(WORLD) if w != c and topo.host(w) == topo.host(c) and topo.chip(w) == topo.chip(c)]
+        near[r] = [w for w in mates if topo.die(w) == topo.die(c)]
+        far[r] = [w for w in mates if topo.die(w) != topo.die(c)]
+    own = {r: (near[r][0], far[r][0], far[r][2]) for r in range(n)}
+    oth = {r: (near[r][1], far[r][1], far[r][3]) for r in range(n)}
+
+    calls, inc, est, busy = {}, {}, {}, {}
+
+    def send(src, ready, transfers):
+        for buf, lo, hi, slot, dests, eng in transfers:
+            width = (hi - lo) * (4 if buf == "q" else 1)
+            t = max([ready] + [busy.get((src, e), 0) for e in eng])
+            for d in dests:
+                t += (128 // len(eng)) * (ROW + width)
+                inc[(d, slot)] = inc.get((d, slot), 0) + len(eng)
+                est[(d, slot)] = max(est.get((d, slot), 0), t)
+            for e in eng:
+                busy[(src, e)] = t
+        calls.setdefault(src, []).append(transfers)
+
+    def turn(r, steps):
+        return [cores[at[(rk[r], (pos[r] + k) % per)]] for k in steps]
+
+    direct = list(range(per - DIRECT, per))
+    fwd = direct[len(direct) - FORWARD:]
+    for r, c in enumerate(cores):
+        p = partner[r]
+        off = _bits(topo.mask(c, cores[p]))
+        on = [e for e in _bits(topo.mask(c, own[r][0])) if e not in off]
+        lo = r * SLOT
+        h, k = len(on) // 2, len(off) // 2
+        send(c, 0, [("q", lo, lo + HALF, r, [own[r][0]], on[:h]), ("q", lo + HALF, lo + SLOT, r, [own[r][1]], on[h:]),
+                    ("q", lo, lo + HALF, r, [oth[p][0]], off[:k]), ("q", lo + HALF, lo + SLOT, r, [oth[p][1]], off[k:])])
+        send(c, 0, [("s", lo, lo + SLOT, r, [own[r][2]], on), ("s", lo, lo + SLOT, r, [oth[p][2]] + turn(r, direct), off)])
+        if direct:
+            send(c, 0, [("q", lo, lo + SLOT, r, turn(r, direct), off)])
+    for r, c in enumerate(cores):
+        p = partner[r]
+        for who, t, dests in ((own[r], r, turn(r, range(1, per - DIRECT))),
+                              (oth[r], p, [c] + turn(r, [k for k in range(1, per) if k not in fwd]))):
+            lo = t * SLOT
+            for w, (buf, a, b) in zip(who, (("q", lo, lo + HALF), ("q", lo + HALF, lo + SLOT), ("s", lo, lo + SLOT))):
+                m = topo.mask(w, dests[0])
+                for d in dests:
+                    m &= topo.mask(w, d)
+                send(w, est[(w, t)] + HOP, [(buf, a, b, t, dests, _bits(m))])
+    for r, c in enumerate(cores):
+        off = _bits(topo.mask(c, cores[partner[r]]))
+        for k in sorted(fwd, key=lambda k: est[(c, at[(rk[r], (pos[r] - k) % per)])]):
+            t = at[(rk[r], (pos[r] - k) % per)]
+            send(c, est[(c, t)] + HOP // 2, [("q", t * SLOT, (t + 1) * SLOT, t, [cores[partner[r]]], off)])
+            send(c, est[(c, t)] + HOP // 2, [("s", t * SLOT, (t + 1) * SLOT, t, [cores[partner[r]]], off)])
+    return calls, inc, est
+
+
+def rank_program(g, core, T, topo):
+    if "plan" not in _CACHE:
+        _CACHE["plan"] = _build(list(T.cores), topo)
+    calls, inc, est = _CACHE["plan"]
+    rank = T.rank_of(core)
+    if rank is None and core not in calls:
+        return
+    sem = T.sem
+
+    def view(buf, lo, hi):
+        return T.q[:, lo:hi].bitcast(dt.uint8) if buf == "q" else T.s[:, lo:hi]
+
+    if rank is not None:
+        lo = rank * SLOT
+        g.sync.dma_start(T.cb[:], T.c[:]).then_inc(sem.ldc, 16)
+        g.scalar.dma_start(T.xb[:], T.x[:]).then_inc(sem.ldx, 16)
+        g.vector.wait_ge(sem.ldc, 16)
+        g.vector.quantize_mx(T.q[:, lo:lo + HALF], T.s[:, lo:lo + HALF], T.cb[:]).then_inc(sem.qd, 1)
+        g.vector.wait_ge(sem.ldx, 16)
+        g.vector.quantize_mx(T.q[:, lo + HALF:lo + SLOT], T.s[:, lo + HALF:lo + SLOT], T.xb[:]).then_inc(sem.qd, 1)
+
+    seen, left = set(), 0
+    for transfers in calls.get(core, []):
+        for tr in transfers:
+            slot = tr[3]
+            if slot not in seen:
+                seen.add(slot)
+                if slot == rank:
+                    g.wait_ge(sem.qd, 2)
+                else:
+                    g.wait_ge(sem["a%d" % slot], inc[(core, slot)])
+        out = []
+        for buf, lo, hi, slot, dests, eng in transfers:
+            ids = []
+            for d in dests:
+                rid, pid = topo.addr(d, core)
+                ids.append(DstId(rid=rid, pnc=pid))
+            out.append(RemoteDMATransfer(dst_ids=ids, dma_engine_mask=sum(1 << e for e in eng), remote_sem=sem["a%d" % slot],
+                                         srcs=[view(buf, lo, hi)], dsts=[view(buf, lo, hi) for d in dests]))
+            left += len(eng)
+        g.remote_dma_fused(out, local_sem=sem.sent)
+    if left:
+        g.wait_ge(sem.sent, left)
+    if rank is None:
+        return
+
+    when = {j: (0 if j == rank else est[(core, j)]) for j in range(N)}
+    pairs = sorted(range(N), key=lambda k: (max(when[k], when[(rank - k) % N]), k))
+    have = set()
+    for i, k in enumerate(pairs):
+        j = (rank - k) % N
+        for t in sorted({k, j}, key=lambda t: when[t]):
+            if t not in have:
+                have.add(t)
+                if t == rank:
+                    g.tensor.wait_ge(sem.qd, 2)
+                else:
+                    g.tensor.wait_ge(sem["a%d" % t], inc[(core, t)])
+        mm = g.tensor.matmul_mx(T.acc[:, 0:HALF], T.q[:, k * SLOT:k * SLOT + HALF], T.s[:, k * SLOT:k * SLOT + HALF],
+                                T.q[:, j * SLOT + HALF:(j + 1) * SLOT], T.s[:, j * SLOT + HALF:(j + 1) * SLOT],
+                                i == 0, i == N - 1)
+    mm.then_inc(sem.mm, 1)
+    g.vector.wait_ge(sem.mm, 1)
+    g.vector.tensor_copy(T.yb[:], T.acc[:, 0:HALF]).then_inc(sem.cp, 1)
+    g.sync.wait_ge(sem.cp, 1)
+    g.sync.dma_start(T.y[:], T.yb[:]).then_inc(sem.st, 16)
+    g.sync.wait_ge(sem.st, 16)

@@ -5,8 +5,9 @@ N = 16
 WORLD = 512
 HALF = 128
 SLOT = 2 * HALF
-DIRECT = 2
-FORWARD = 2
+DIRECT = 0
+FORWARD = 0
+PDIRECT = False
 
 SCRATCH = {
     "cb": ("sbuf", [128, 4 * HALF], "bfloat16"),
@@ -47,8 +48,8 @@ def _build(cores, topo):
         mates = [w for w in range(WORLD) if w != c and topo.host(w) == topo.host(c) and topo.chip(w) == topo.chip(c)]
         near[r] = [w for w in mates if topo.die(w) == topo.die(c)]
         far[r] = [w for w in mates if topo.die(w) != topo.die(c)]
-    own = {r: (near[r][0], far[r][0], far[r][2]) for r in range(n)}
-    oth = {r: (near[r][1], far[r][1], far[r][3]) for r in range(n)}
+    own = {r: (near[r][0], far[r][0], near[r][2]) for r in range(n)}
+    oth = {r: (near[r][1], far[r][1], far[r][2]) for r in range(n)}
 
     calls, inc, est, busy = {}, {}, {}, {}
 
@@ -75,16 +76,23 @@ def _build(cores, topo):
         on = [e for e in _bits(topo.mask(c, own[r][0])) if e not in off]
         lo = r * SLOT
         h, k = len(on) // 2, len(off) // 2
-        send(c, 0, [("q", lo, lo + HALF, r, [own[r][0]], on[:h]), ("q", lo + HALF, lo + SLOT, r, [own[r][1]], on[h:]),
-                    ("q", lo, lo + HALF, r, [oth[p][0]], off[:k]), ("q", lo + HALF, lo + SLOT, r, [oth[p][1]], off[k:])])
-        send(c, 0, [("s", lo, lo + SLOT, r, [own[r][2]], on), ("s", lo, lo + SLOT, r, [oth[p][2]] + turn(r, direct), off)])
-        if direct:
-            send(c, 0, [("q", lo, lo + SLOT, r, turn(r, direct), off)])
+        mine = ([cores[p]] if PDIRECT else []) + turn(r, direct)
+        use_own, use_oth = DIRECT < per - 1, not (PDIRECT and FORWARD == per - 1)
+        first = ([("q", lo, lo + HALF, r, [own[r][0]], on[:h]), ("q", lo + HALF, lo + SLOT, r, [own[r][1]], on[h:])] if use_own else []) + \
+                ([("q", lo, lo + HALF, r, [oth[p][0]], off[:k]), ("q", lo + HALF, lo + SLOT, r, [oth[p][1]], off[k:])] if use_oth else [])
+        if first:
+            send(c, 0, first)
+        send(c, 0, ([("s", lo, lo + SLOT, r, [own[r][2]], on)] if use_own else []) +
+             [("s", lo, lo + SLOT, r, ([oth[p][2]] if use_oth else []) + mine, off)])
+        if mine:
+            send(c, 0, [("q", lo, lo + SLOT, r, mine, off)])
     for r, c in enumerate(cores):
         p = partner[r]
         for who, t, dests in ((own[r], r, turn(r, range(1, per - DIRECT))),
-                              (oth[r], p, [c] + turn(r, [k for k in range(1, per) if k not in fwd]))):
+                              (oth[r], p, ([] if PDIRECT else [c]) + turn(r, [k for k in range(1, per) if k not in fwd]))):
             lo = t * SLOT
+            if not dests:
+                continue
             for w, (buf, a, b) in zip(who, (("q", lo, lo + HALF), ("q", lo + HALF, lo + SLOT), ("s", lo, lo + SLOT))):
                 m = topo.mask(w, dests[0])
                 for d in dests:

from concourse.bass import DstId, RemoteDMATransfer
from concourse.mybir import dt

N = 16
WORLD = 512
HALF = 128
SLOT = 2 * HALF
DIRECT = 0
FORWARD = 0
PDIRECT = False

SCRATCH = {
    "cb": ("sbuf", [128, 4 * HALF], "bfloat16"),
    "xb": ("sbuf", [128, 4 * HALF], "bfloat16"),
    "q": ("sbuf", [128, N * SLOT], "float8_e4m3fn_x4"),
    "s": ("sbuf", [128, N * SLOT], "uint8"),
    "yb": ("sbuf", [128, HALF], "float32"),
    "acc": ("psum", [128, 512], "float32"),
}
SEMAPHORES = ["ldc", "ldx", "qd", "sent", "mm", "cp", "st"] + ["a%d" % j for j in range(N)]

ROW, HOP = 512, 60000

_CACHE = {}


def _bits(m):
    return [i for i in range(16) if (m >> i) & 1]


def _build(cores, topo):
    n = len(cores)
    rk = [topo.rack(topo.host(c)) for c in cores]
    partner = {}
    for r, c in enumerate(cores):
        for r2, c2 in enumerate(cores):
            if rk[r2] != rk[r] and topo.chip(c2) == topo.chip(c) and topo.may_write(c, c2):
                partner[r] = r2
    pos, at = {}, {}
    for i, r in enumerate([r for r in range(n) if rk[r] == rk[0]]):
        pos[r] = i
        pos[partner[r]] = i
    for r in range(n):
        at[(rk[r], pos[r])] = r
    per = n // 2
    near, far = {}, {}
    for r, c in enumerate(cores):
        mates = [w for w in range(WORLD) if w != c and topo.host(w) == topo.host(c) and topo.chip(w) == topo.chip(c)]
        near[r] = [w for w in mates if topo.die(w) == topo.die(c)]
        far[r] = [w for w in mates if topo.die(w) != topo.die(c)]
    own = {r: (near[r][0], far[r][0], near[r][2]) for r in range(n)}
    oth = {r: (near[r][1], far[r][1], far[r][2]) for r in range(n)}

    calls, inc, est, busy = {}, {}, {}, {}

    def send(src, ready, transfers):
        for buf, lo, hi, slot, dests, eng in transfers:
            width = (hi - lo) * (4 if buf == "q" else 1)
            t = max([ready] + [busy.get((src, e), 0) for e in eng])
            for d in dests:
                t += (128 // len(eng)) * (ROW + width)
                inc[(d, slot)] = inc.get((d, slot), 0) + len(eng)
                est[(d, slot)] = max(est.get((d, slot), 0), t)
            for e in eng:
                busy[(src, e)] = t
        calls.setdefault(src, []).append(transfers)

    def turn(r, steps):
        return [cores[at[(rk[r], (pos[r] + k) % per)]] for k in steps]

    direct = list(range(per - DIRECT, per))
    fwd = direct[len(direct) - FORWARD:]
    for r, c in enumerate(cores):
        p = partner[r]
        off = _bits(topo.mask(c, cores[p]))
        on = [e for e in _bits(topo.mask(c, own[r][0])) if e not in off]
        lo = r * SLOT
        h, k = len(on) // 2, len(off) // 2
        mine = ([cores[p]] if PDIRECT else []) + turn(r, direct)
        use_own, use_oth = DIRECT < per - 1, not (PDIRECT and FORWARD == per - 1)
        first = ([("q", lo, lo + HALF, r, [own[r][0]], on[:h]), ("q", lo + HALF, lo + SLOT, r, [own[r][1]], on[h:])] if use_own else []) + \
                ([("q", lo, lo + HALF, r, [oth[p][0]], off[:k]), ("q", lo + HALF, lo + SLOT, r, [oth[p][1]], off[k:])] if use_oth else [])
        if first:
            send(c, 0, first)
        send(c, 0, ([("s", lo, lo + SLOT, r, [own[r][2]], on)] if use_own else []) +
             [("s", lo, lo + SLOT, r, ([oth[p][2]] if use_oth else []) + mine, off)])
        if mine:
            send(c, 0, [("q", lo, lo + SLOT, r, mine, off)])
    for r, c in enumerate(cores):
        p = partner[r]
        for who, t, dests in ((own[r], r, turn(r, range(1, per - DIRECT))),
                              (oth[r], p, ([] if PDIRECT else [c]) + turn(r, [k for k in range(1, per) if k not in fwd]))):
            lo = t * SLOT
            if not dests:
                continue
            for w, (buf, a, b) in zip(who, (("q", lo, lo + HALF), ("q", lo + HALF, lo + SLOT), ("s", lo, lo + SLOT))):
                m = topo.mask(w, dests[0])
                for d in dests:
                    m &= topo.mask(w, d)
                send(w, est[(w, t)] + HOP, [(buf, a, b, t, dests, _bits(m))])
    for r, c in enumerate(cores):
        off = _bits(topo.mask(c, cores[partner[r]]))
        for k in sorted(fwd, key=lambda k: est[(c, at[(rk[r], (pos[r] - k) % per)])]):
            t = at[(rk[r], (pos[r] - k) % per)]
            send(c, est[(c, t)] + HOP // 2, [("q", t * SLOT, (t + 1) * SLOT, t, [cores[partner[r]]], off)])
            send(c, est[(c, t)] + HOP // 2, [("s", t * SLOT, (t + 1) * SLOT, t, [cores[partner[r]]], off)])
    return calls, inc, est


def rank_program(g, core, T, topo):
    if "plan" not in _CACHE:
        _CACHE["plan"] = _build(list(T.cores), topo)
    calls, inc, est = _CACHE["plan"]
    rank = T.rank_of(core)
    if rank is None and core not in calls:
        return
    sem = T.sem

    def view(buf, lo, hi):
        return T.q[:, lo:hi].bitcast(dt.uint8) if buf == "q" else T.s[:, lo:hi]

    if rank is not None:
        lo = rank * SLOT
        g.sync.dma_start(T.cb[:], T.c[:]).then_inc(sem.ldc, 16)
        g.scalar.dma_start(T.xb[:], T.x[:]).then_inc(sem.ldx, 16)
        g.vector.wait_ge(sem.ldc, 16)
        g.vector.quantize_mx(T.q[:, lo:lo + HALF], T.s[:, lo:lo + HALF], T.cb[:]).then_inc(sem.qd, 1)
        g.vector.wait_ge(sem.ldx, 16)
        g.vector.quantize_mx(T.q[:, lo + HALF:lo + SLOT], T.s[:, lo + HALF:lo + SLOT], T.xb[:]).then_inc(sem.qd, 1)

    seen, left = set(), 0
    for transfers in calls.get(core, []):
        for tr in transfers:
            slot = tr[3]
            if slot not in seen:
                seen.add(slot)
                if slot == rank:
                    g.wait_ge(sem.qd, 2)
                else:
                    g.wait_ge(sem["a%d" % slot], inc[(core, slot)])
        out = []
        for buf, lo, hi, slot, dests, eng in transfers:
            ids = []
            for d in dests:
                rid, pid = topo.addr(d, core)
                ids.append(DstId(rid=rid, pnc=pid))
            out.append(RemoteDMATransfer(dst_ids=ids, dma_engine_mask=sum(1 << e for e in eng), remote_sem=sem["a%d" % slot],
                                         srcs=[view(buf, lo, hi)], dsts=[view(buf, lo, hi) for d in dests]))
            left += len(eng)
        g.remote_dma_fused(out, local_sem=sem.sent)
    if left:
        g.wait_ge(sem.sent, left)
    if rank is None:
        return

    when = {j: (0 if j == rank else est[(core, j)]) for j in range(N)}
    pairs = sorted(range(N), key=lambda k: (max(when[k], when[(rank - k) % N]), k))
    have = set()
    for i, k in enumerate(pairs):
        j = (rank - k) % N
        for t in sorted({k, j}, key=lambda t: when[t]):
            if t not in have:
                have.add(t)
                if t == rank:
                    g.tensor.wait_ge(sem.qd, 2)
                else:
                    g.tensor.wait_ge(sem["a%d" % t], inc[(core, t)])
        mm = g.tensor.matmul_mx(T.acc[:, 0:HALF], T.q[:, k * SLOT:k * SLOT + HALF], T.s[:, k * SLOT:k * SLOT + HALF],
                                T.q[:, j * SLOT + HALF:(j + 1) * SLOT], T.s[:, j * SLOT + HALF:(j + 1) * SLOT],
                                i == 0, i == N - 1)
    mm.then_inc(sem.mm, 1)
    g.vector.wait_ge(sem.mm, 1)
    g.vector.tensor_copy(T.yb[:], T.acc[:, 0:HALF]).then_inc(sem.cp, 1)
    g.sync.wait_ge(sem.cp, 1)
    g.sync.dma_start(T.y[:], T.yb[:]).then_inc(sem.st, 16)
    g.sync.wait_ge(sem.st, 16)
